import numpy as np, ml_dtypes
CORES = [33,34,161,162,289,290,417,418]
N = 8
NH, QP = 8, 128
def setup_inputs(rng):
    return {"q": rng.standard_normal((N, 128, NH * QP), dtype=np.float32).astype(ml_dtypes.bfloat16), "k": rng.standard_normal((N, 128, NH * 128), dtype=np.float32).astype(ml_dtypes.bfloat16), "v": rng.standard_normal((N, 128, NH * 128), dtype=np.float32).astype(ml_dtypes.bfloat16)}
def setup_inputs_big(rng):
    d = setup_inputs(rng)
    for k in ("q", "k", "v"): d[k] = (d[k].astype(np.float32) * 1024.0).astype(d[k].dtype)
    return d
def setup_inputs_small(rng):
    d = setup_inputs(rng)
    for k in ("q", "k", "v"): d[k] = (d[k].astype(np.float32) * (1 / 1024.0)).astype(d[k].dtype)
    return d
def setup_inputs_apart(rng):
    d = setup_inputs(rng)
    f = (10.0 ** rng.permutation(np.linspace(-1.5, 1.5, N))).astype(np.float32).reshape(N, 1, 1)
    for k in ("q", "k", "v"): d[k] = (d[k].astype(np.float32) * f).astype(d[k].dtype)
    return d
def reference(q, k, v):
    Q, K, V = q.astype(np.float64), k.astype(np.float64), v.astype(np.float64)
    y = np.zeros((N, 128, NH * QP))
    for r in range(N):
        for h in range(NH):
            for j in range(N):
                S = np.maximum(K[j][:, 128 * h:128 * h + 128].T @ Q[r][:, QP * h:QP * h + QP], 0.0)
                y[r][:, QP * h:QP * h + QP] += V[j][:, 128 * h:128 * h + 128].T @ S
    return {"y": y.astype(ml_dtypes.bfloat16 if q.dtype != np.float64 else np.float64)}

@@ -1,0 +1,208 @@
+from concourse.bass import DstId, RemoteDMATransfer
+from concourse.mybir import AluOpType
+
+W = 256
+P = 128
+NB = 4
+
+SCRATCH = {
+    "qin": ("sbuf", [128, 1024], "bfloat16"),
+    "kin": ("sbuf", [128, 1024], "bfloat16"),
+    "vin": ("sbuf", [128, 1024], "bfloat16"),
+    "qland": ("sbuf", [128, 3 * W], "bfloat16"),
+    "kland": ("sbuf", [128, 7 * W], "bfloat16"),
+    "vland": ("sbuf", [128, 7 * W], "bfloat16"),
+    "ssb": ("sbuf", [128, NB * 512], "bfloat16"),
+    "zeros": ("sbuf", [128, 512], "float32"),
+    "osb": ("sbuf", [128, 3 * W], "bfloat16"),
+    "ybuf": ("sbuf", [128, 1024], "bfloat16"),
+    "s0": ("psum", [128, 512], "float32"), "s1": ("psum", [128, 512], "float32"),
+    "s2": ("psum", [128, 512], "float32"), "s3": ("psum", [128, 512], "float32"),
+    "o0": ("psum", [128, 512], "float32"), "o1": ("psum", [128, 512], "float32"),
+    "o2": ("psum", [128, 512], "float32"), "o3": ("psum", [128, 512], "float32"),
+}
+SEMAPHORES = (["ldA", "ldB", "ldC", "sent", "aqp", "aqc", "zs", "ocf", "ocp", "oco", "ayc", "ayp", "st"]
+              + ["akv%d" % i for i in range(1, 8)]
+              + ["sd%d" % b for b in range(NB)] + ["rd%d" % b for b in range(NB)] + ["od%d" % b for b in range(NB)])
+
+KV_ENG = {1: 2, 2: 2, 3: 2, 4: 2, 5: 2, 6: 2, 7: 4}
+
+
+def _bits(m):
+    return [e for e in range(m.bit_length()) if (m >> e) & 1]
+
+
+def _mask(es):
+    m = 0
+    for e in es:
+        m |= 1 << e
+    return m
+
+
+def _plan(c, cores, topo):
+    here = [d for d in cores if topo.host(d) == topo.host(c)]
+    pos = here.index(c)
+    rack = topo.rack(topo.host(c))
+    M = [d for d in cores if topo.same_plane(c, d)]
+    C = [d for d in cores if topo.rack(topo.host(d)) != rack and topo.may_write(c, d)]
+    D = [d for d in cores if not topo.may_write(c, d)]
+    return {
+        "pos": pos, "rack": rack, "hp": 2 * rack + pos, "partner": here[1 - pos], "M": M, "C": C, "D": D,
+        "order": [c, here[1 - pos], M[pos], C[pos], M[1 - pos], D[pos], C[1 - pos], D[1 - pos]],
+        "slots": [here[0], here[1], C[0], C[1]],
+    }
+
+
+def rank_program(g, core, T, topo):
+    if T.rank_of(core) is None:
+        return
+    cores = list(T.cores)
+    me = _plan(core, cores, topo)
+    pos, partner, M, C = me["pos"], me["partner"], me["M"], me["C"]
+    S = T.sem
+    near, far = 512 * me["rack"], 512 * (1 - me["rack"])
+    mycol = W * me["hp"]
+
+    off = _bits(topo.mask(core, C[0]) & topo.mask(core, M[0]))
+    on = [e for e in _bits(topo.mask(core, partner)) if e not in off]
+    cab, sw = off[0::2], off[1::2]
+    sent = [0]
+
+    def xfer(dst, src_ap, dst_ap, engines, sem):
+        rid, pid = topo.addr(dst, core)
+        sent[0] += len(engines)
+        return RemoteDMATransfer(dst_ids=[DstId(rid=rid, pnc=pid)], dma_engine_mask=_mask(engines), remote_sem=sem,
+                                 src=src_ap, dst=dst_ap)
+
+    def kv_to(dst, source, k_ap, v_ap, engines):
+        idx = _plan(dst, cores, topo)["order"].index(source)
+        n = KV_ENG[idx]
+        c0 = (idx - 1) * W
+        return [xfer(dst, k_ap, T.kland[:, c0:c0 + W], engines[0:n], S["akv%d" % idx]),
+                xfer(dst, v_ap, T.vland[:, c0:c0 + W], engines[n:2 * n], S["akv%d" % idx])]
+
+    def own_kv_to(dst, engines):
+        c0 = W * _plan(dst, cores, topo)["hp"]
+        return kv_to(dst, core, T.kin[:, c0:c0 + W], T.vin[:, c0:c0 + W], engines)
+
+    def q_to(dst, engines):
+        pl = _plan(dst, cores, topo)
+        c0 = W * pl["hp"]
+        slot = pl["slots"].index(core)
+        if dst == partner:
+            return xfer(dst, T.qin[:, c0:c0 + W], T.qland[:, 0:W], engines, S.aqp)
+        return xfer(dst, T.qin[:, c0:c0 + W], T.qland[:, (slot - 1) * W:slot * W], engines, S.aqc)
+
+    g.sync.dma_start(T.kin[:, far:far + 512], T.k[:, far:far + 512]).then_inc(S.ldA, 16)
+    g.scalar.dma_start(T.vin[:, far:far + 512], T.v[:, far:far + 512]).then_inc(S.ldA, 16)
+    g.sync.dma_start(T.kin[:, near:near + 512], T.k[:, near:near + 512]).then_inc(S.ldB, 16)
+    g.scalar.dma_start(T.vin[:, near:near + 512], T.v[:, near:near + 512]).then_inc(S.ldB, 16)
+    g.scalar.dma_start(T.qin[:, near:near + 512], T.q[:, near:near + 512]).then_inc(S.ldB, 16)
+    g.sync.dma_start(T.qin[:, far:far + 512], T.q[:, far:far + 512]).then_inc(S.ldC, 16)
+    g.vector.memset(T.zeros[:, :], 0.0).then_inc(S.zs, 1)
+
+    g.wait_ge(S.ldA, 32)
+    g.remote_dma_fused(own_kv_to(C[pos], cab), local_sem=S.sent)
+    g.wait_ge(S.ldB, 48)
+    g.remote_dma_fused(own_kv_to(M[pos], sw) + own_kv_to(partner, on[2:6]) + [q_to(partner, on[0:2])], local_sem=S.sent)
+    g.wait_ge(S.ldC, 16)
+    g.remote_dma_fused([q_to(C[0], cab[0:2]), q_to(C[1], cab[2:4])] + own_kv_to(M[1 - pos], sw), local_sem=S.sent)
+    g.remote_dma_fused(own_kv_to(C[1 - pos], cab), local_sem=S.sent)
+    for src, engines in ((C[pos], sw), (C[1 - pos], cab + sw)):
+        idx = me["order"].index(src)
+        c0 = (idx - 1) * W
+        g.wait_ge(S["akv%d" % idx], 2 * KV_ENG[idx])
+        g.remote_dma_fused(kv_to(M[pos], src, T.kland[:, c0:c0 + W], T.vland[:, c0:c0 + W], engines), local_sem=S.sent)
+
+    units = [(0, 0), (1, 0), (2, 0), (0, 1), (1, 1), (2, 1)] + [(j, h) for j in range(3, 8) for h in (1, 0)]
+    nu = len(units)
+    sbank = [T.s0, T.s1, T.s2, T.s3]
+    oacc = [[T.o0, T.o1], [T.o2, T.o3]]
+    seen = set()
+    first = {0: min(u for u in range(nu) if units[u][1] == 0), 1: min(u for u in range(nu) if units[u][1] == 1)}
+    last = {0: max(u for u in range(nu) if units[u][1] == 0), 1: max(u for u in range(nu) if units[u][1] == 1)}
+
+    def twait(name, val):
+        if name not in seen:
+            seen.add(name)
+            g.tensor.wait_ge(S[name], val)
+
+    def k_of(j, h):
+        if j == 0:
+            return T.kin[:, mycol + P * h:mycol + P * h + P]
+        return T.kland[:, (j - 1) * W + P * h:(j - 1) * W + P * h + P]
+
+    def v_of(j, h):
+        if j == 0:
+            return T.vin[:, mycol + P * h:mycol + P * h + P]
+        return T.vland[:, (j - 1) * W + P * h:(j - 1) * W + P * h + P]
+
+    def q_of(slot, h):
+        if me["slots"][slot] == core:
+            return T.qin[:, mycol + P * h:mycol + P * h + P]
+        c0 = 0 if slot < 2 else (slot - 1) * W
+        return T.qland[:, c0 + P * h:c0 + P * h + P]
+
+    def emit_s(u):
+        j, half = units[u]
+        b = u % NB
+        if j == 0:
+            twait("ldB", 48)
+        else:
+            twait("akv%d" % j, 2 * KV_ENG[j])
+        if half == 0:
+            twait("ldB", 48)
+            twait("aqp", 2)
+        else:
+            twait("aqc", 4)
+        for h in (0, 1):
+            for s in (0, 1):
+                c0 = W * h + P * s
+                g.tensor.matmul(sbank[b][:, c0:c0 + P], k_of(j, h), q_of(2 * half + s, h), True, True).then_inc(S["sd%d" % b], 1)
+
+    def emit_o(u):
+        j, half = units[u]
+        b = u % NB
+        g.tensor.wait_ge(S["rd%d" % b], u // NB + 1)
+        for h in (0, 1):
+            g.tensor.matmul(oacc[half][h][:, 0:W], v_of(j, h), T.ssb[:, 512 * b + W * h:512 * b + W * h + W],
+                            u == first[half], u == last[half]).then_inc(S["od%d" % b], 1)
+
+    emit_s(0)
+    for u in range(nu):
+        if u + 1 < nu:
+            emit_s(u + 1)
+        emit_o(u)
+
+    g.vector.wait_ge(S.zs, 1)
+    for u in range(nu):
+        b = u % NB
+        g.vector.wait_ge(S["sd%d" % b], 4 * (u // NB + 1))
+        if u >= NB:
+            g.vector.wait_ge(S["od%d" % b], 2 * (u // NB))
+        g.vector.tensor_tensor(T.ssb[:, 512 * b:512 * b + 512], sbank[b][:, :], T.zeros[:, :], AluOpType.max).then_inc(S["rd%d" % b], 1)
+    for u in range(nu - NB, nu - 1):
+        g.vector.wait_ge(S["od%d" % (u % NB)], 2 * (u // NB + 1))
+    for s in (0, 1):
+        for h in (0, 1):
+            g.vector.tensor_copy(T.osb[:, W * (s + 1) + P * h:W * (s + 1) + P * h + P], oacc[1][h][:, P * s:P * s + P]).then_inc(S.ocf, 1)
+    g.vector.wait_ge(S["od%d" % ((nu - 1) % NB)], 2 * ((nu - 1) // NB + 1))
+    for h in (0, 1):
+        g.vector.tensor_copy(T.osb[:, P * h:P * h + P], oacc[0][h][:, P * (1 - pos):P * (1 - pos) + P]).then_inc(S.ocp, 1)
+    for h in (0, 1):
+        g.vector.tensor_copy(T.ybuf[:, mycol + P * h:mycol + P * h + P], oacc[0][h][:, P * pos:P * pos + P]).then_inc(S.oco, 1)
+
+    g.wait_ge(S.ocf, 4)
+    g.remote_dma_fused([xfer(C[0], T.osb[:, W:2 * W], T.ybuf[:, mycol:mycol + W], off[0:4], S.ayc),
+                        xfer(C[1], T.osb[:, 2 * W:3 * W], T.ybuf[:, mycol:mycol + W], off[4:8], S.ayc)], local_sem=S.sent)
+    g.wait_ge(S.ocp, 2)
+    g.remote_dma_fused([xfer(partner, T.osb[:, 0:W], T.ybuf[:, mycol:mycol + W], on[0:4], S.ayp)], local_sem=S.sent)
+
+    g.sync.wait_ge(S.oco, 2)
+    g.sync.wait_ge(S.ayp, 4)
+    g.sync.dma_start(T.y[:, near:near + 512], T.ybuf[:, near:near + 512]).then_inc(S.st, 16)
+    g.scalar.wait_ge(S.ayc, 8)
+    g.scalar.dma_start(T.y[:, far:far + 512], T.ybuf[:, far:far + 512]).then_inc(S.st, 16)
+
+    g.wait_ge(S.sent, sent[0])
+    g.wait_ge(S.st, 32)

@@ -1,31 +1,32 @@
 from concourse.bass import DstId, RemoteDMATransfer
 from concourse.mybir import AluOpType
 
-W = 256
+WORLD = 512
 P = 128
-NB = 4
+NH = 8
 
 SCRATCH = {
     "qin": ("sbuf", [128, 1024], "bfloat16"),
     "kin": ("sbuf", [128, 1024], "bfloat16"),
     "vin": ("sbuf", [128, 1024], "bfloat16"),
-    "qland": ("sbuf", [128, 3 * W], "bfloat16"),
-    "kland": ("sbuf", [128, 7 * W], "bfloat16"),
-    "vland": ("sbuf", [128, 7 * W], "bfloat16"),
-    "ssb": ("sbuf", [128, NB * 512], "bfloat16"),
+    "qb": ("sbuf", [128, 4 * P], "bfloat16"),
+    "kb": ("sbuf", [128, 4 * P], "bfloat16"),
+    "vb": ("sbuf", [128, 4 * P], "bfloat16"),
+    "ssb": ("sbuf", [128, 4 * 512], "bfloat16"),
     "zeros": ("sbuf", [128, 512], "float32"),
-    "osb": ("sbuf", [128, 3 * W], "bfloat16"),
-    "ybuf": ("sbuf", [128, 1024], "bfloat16"),
+    "osb": ("sbuf", [128, 4 * P], "bfloat16"),
+    "ya": ("sbuf", [128, 1024], "bfloat16"),
+    "yb": ("sbuf", [128, 1024], "bfloat16"),
+    "ys": ("sbuf", [128, 1024], "bfloat16"),
     "s0": ("psum", [128, 512], "float32"), "s1": ("psum", [128, 512], "float32"),
     "s2": ("psum", [128, 512], "float32"), "s3": ("psum", [128, 512], "float32"),
-    "o0": ("psum", [128, 512], "float32"), "o1": ("psum", [128, 512], "float32"),
-    "o2": ("psum", [128, 512], "float32"), "o3": ("psum", [128, 512], "float32"),
+    "o": ("psum", [128, 512], "float32"),
 }
-SEMAPHORES = (["ldA", "ldB", "ldC", "sent", "aqp", "aqc", "zs", "ocf", "ocp", "oco", "ayc", "ayp", "st"]
-              + ["akv%d" % i for i in range(1, 8)]
-              + ["sd%d" % b for b in range(NB)] + ["rd%d" % b for b in range(NB)] + ["od%d" % b for b in range(NB)])
+SEMAPHORES = (["ldq", "ldk", "ldv", "sent", "zs", "od", "oc", "own", "ay0", "ay1", "yd0", "yd1", "st"]
+              + ["n" + x for x in "qkv"] + ["f" + x for x in "qkv"]
+              + ["sd%d" % j for j in range(4)] + ["rd%d" % j for j in range(4)])
 
-KV_ENG = {1: 2, 2: 2, 3: 2, 4: 2, 5: 2, 6: 2, 7: 4}
+E_DEAL, E_OWN = 2, 1
 
 
 def _bits(m):
@@ -39,33 +40,42 @@ def _mask(es):
     return m
 
 
-def _plan(c, cores, topo):
-    here = [d for d in cores if topo.host(d) == topo.host(c)]
-    pos = here.index(c)
-    rack = topo.rack(topo.host(c))
-    M = [d for d in cores if topo.same_plane(c, d)]
-    C = [d for d in cores if topo.rack(topo.host(d)) != rack and topo.may_write(c, d)]
-    D = [d for d in cores if not topo.may_write(c, d)]
-    return {
-        "pos": pos, "rack": rack, "hp": 2 * rack + pos, "partner": here[1 - pos], "M": M, "C": C, "D": D,
-        "order": [c, here[1 - pos], M[pos], C[pos], M[1 - pos], D[pos], C[1 - pos], D[1 - pos]],
-        "slots": [here[0], here[1], C[0], C[1]],
-    }
+def _layout(cores, topo):
+    L = {}
+    for H in sorted({topo.host(c) for c in cores}):
+        ranks = [c for c in cores if topo.host(c) == H]
+        r0 = ranks[0]
+        chip = [c for c in range(WORLD) if topo.host(c) == H and topo.chip(c) == topo.chip(r0)]
+        a = [c for c in chip if topo.die(c) == topo.die(r0)]
+        b = [c for c in chip if topo.die(c) != topo.die(r0)]
+        work = []
+        for x, y in zip(a, b):
+            work += [x, y]
+        mate = [topo.host(d) for d in cores if topo.same_plane(r0, d)][0]
+        cable = [topo.host(d) for d in cores if topo.rack(topo.host(d)) != topo.rack(H) and topo.may_write(r0, d)][0]
+        L[H] = {"ranks": ranks, "work": work, "mate": mate, "cable": cable}
+    return L
 
 
 def rank_program(g, core, T, topo):
-    if T.rank_of(core) is None:
-        return
     cores = list(T.cores)
-    me = _plan(core, cores, topo)
-    pos, partner, M, C = me["pos"], me["partner"], me["M"], me["C"]
+    L = _layout(cores, topo)
+    H = topo.host(core)
+    if H not in L or core not in L[H]["work"]:
+        return
+    me = L[H]
+    mate, cable = L[me["mate"]], L[me["cable"]]
+    head = me["work"].index(core)
+    hc = P * head
+    is_rank = T.rank_of(core) is not None
+    pos = me["ranks"].index(core) if is_rank else None
     S = T.sem
-    near, far = 512 * me["rack"], 512 * (1 - me["rack"])
-    mycol = W * me["hp"]
+    askers = me["ranks"] + mate["ranks"]
+    other = {"q": mate, "k": cable, "v": cable}
+    land = {"q": T.qb, "k": T.kb, "v": T.vb}
 
-    off = _bits(topo.mask(core, C[0]) & topo.mask(core, M[0]))
-    on = [e for e in _bits(topo.mask(core, partner)) if e not in off]
-    cab, sw = off[0::2], off[1::2]
+    off = _bits(topo.mask(core, mate["ranks"][0]) & topo.mask(core, cable["ranks"][0]))
+    on = [e for e in _bits(topo.mask(core, [c for c in me["work"] if c != core][0])) if e not in off]
     sent = [0]
 
     def xfer(dst, src_ap, dst_ap, engines, sem):
@@ -74,135 +84,101 @@ def rank_program(g, core, T, topo):
         return RemoteDMATransfer(dst_ids=[DstId(rid=rid, pnc=pid)], dma_engine_mask=_mask(engines), remote_sem=sem,
                                  src=src_ap, dst=dst_ap)
 
-    def kv_to(dst, source, k_ap, v_ap, engines):
-        idx = _plan(dst, cores, topo)["order"].index(source)
-        n = KV_ENG[idx]
-        c0 = (idx - 1) * W
-        return [xfer(dst, k_ap, T.kland[:, c0:c0 + W], engines[0:n], S["akv%d" % idx]),
-                xfer(dst, v_ap, T.vland[:, c0:c0 + W], engines[n:2 * n], S["akv%d" % idx])]
+    if is_rank:
+        src = {"q": T.qin, "k": T.kin, "v": T.vin}
+        inp = {"q": T.q, "k": T.k, "v": T.v}
+        for x in "qkv":
+            g.sync.dma_start(src[x][:, 0:512], inp[x][:, 0:512]).then_inc(S["ld" + x], 16)
+            g.scalar.dma_start(src[x][:, 512:1024], inp[x][:, 512:1024]).then_inc(S["ld" + x], 16)
+        near, far = slice(pos * P, pos * P + P), slice((2 + pos) * P, (2 + pos) * P + P)
+        duo = [(off + on)[2 * i:2 * i + 2] for i in range(8)]
+        same = [c for c in me["work"] if c != core and topo.die(c) == topo.die(core)]
+        cross = [c for c in me["work"] if topo.die(c) != topo.die(core)]
+        lone = [h for h in range(NH) if me["work"][h] in cores]
+        for ci, x in enumerate("qkv"):
+            a, b, side = [(0, 1, 0), (2, 3, 0), (0, 1, 1)][ci]
+            rest = [duo[i] for i in range(8) if i not in (a, b)]
+            tr = []
+            for i, h in enumerate(lone):
+                tr.append(xfer(other[x]["work"][h], src[x][:, P * h:P * h + P], land[x][:, far], [duo[(a, b)[i]][side]], S["f" + x]))
+            plan = [(cross[3], [duo[a][1 - side], duo[b][1 - side]])]
+            for i in range(3):
+                plan.append((same[i], [rest[2 * i][0], rest[2 * i + 1][0]]))
+                plan.append((cross[i], [rest[2 * i][1], rest[2 * i + 1][1]]))
+            for dst, eng in plan:
+                h = me["work"].index(dst)
+                tr.append(xfer(dst, src[x][:, P * h:P * h + P], land[x][:, near], eng, S["n" + x]))
+            g.wait_ge(S["ld" + x], 32)
+            g.remote_dma_fused(tr, local_sem=S.sent)
+    else:
+        for x in "qkv":
+            g.wait_ge(S["n" + x], 2 * E_DEAL)
+            g.remote_dma_fused([xfer(other[x]["work"][head], land[x][:, 0:2 * P], land[x][:, 2 * P:4 * P], off, S["f" + x])],
+                               local_sem=S.sent)
 
-    def own_kv_to(dst, engines):
-        c0 = W * _plan(dst, cores, topo)["hp"]
-        return kv_to(dst, core, T.kin[:, c0:c0 + W], T.vin[:, c0:c0 + W], engines)
+    n_near = E_DEAL * len([r for r in me["ranks"] if r != core])
+    n_far = {x: (2 * E_OWN if other[x]["work"][head] in cores else len(off)) for x in "qkv"}
 
-    def q_to(dst, engines):
-        pl = _plan(dst, cores, topo)
-        c0 = W * pl["hp"]
-        slot = pl["slots"].index(core)
-        if dst == partner:
-            return xfer(dst, T.qin[:, c0:c0 + W], T.qland[:, 0:W], engines, S.aqp)
-        return xfer(dst, T.qin[:, c0:c0 + W], T.qland[:, (slot - 1) * W:slot * W], engines, S.aqc)
-
-    g.sync.dma_start(T.kin[:, far:far + 512], T.k[:, far:far + 512]).then_inc(S.ldA, 16)
-    g.scalar.dma_start(T.vin[:, far:far + 512], T.v[:, far:far + 512]).then_inc(S.ldA, 16)
-    g.sync.dma_start(T.kin[:, near:near + 512], T.k[:, near:near + 512]).then_inc(S.ldB, 16)
-    g.scalar.dma_start(T.vin[:, near:near + 512], T.v[:, near:near + 512]).then_inc(S.ldB, 16)
-    g.scalar.dma_start(T.qin[:, near:near + 512], T.q[:, near:near + 512]).then_inc(S.ldB, 16)
-    g.sync.dma_start(T.qin[:, far:far + 512], T.q[:, far:far + 512]).then_inc(S.ldC, 16)
-    g.vector.memset(T.zeros[:, :], 0.0).then_inc(S.zs, 1)
-
-    g.wait_ge(S.ldA, 32)
-    g.remote_dma_fused(own_kv_to(C[pos], cab), local_sem=S.sent)
-    g.wait_ge(S.ldB, 48)
-    g.remote_dma_fused(own_kv_to(M[pos], sw) + own_kv_to(partner, on[2:6]) + [q_to(partner, on[0:2])], local_sem=S.sent)
-    g.wait_ge(S.ldC, 16)
-    g.remote_dma_fused([q_to(C[0], cab[0:2]), q_to(C[1], cab[2:4])] + own_kv_to(M[1 - pos], sw), local_sem=S.sent)
-    g.remote_dma_fused(own_kv_to(C[1 - pos], cab), local_sem=S.sent)
-    for src, engines in ((C[pos], sw), (C[1 - pos], cab + sw)):
-        idx = me["order"].index(src)
-        c0 = (idx - 1) * W
-        g.wait_ge(S["akv%d" % idx], 2 * KV_ENG[idx])
-        g.remote_dma_fused(kv_to(M[pos], src, T.kland[:, c0:c0 + W], T.vland[:, c0:c0 + W], engines), local_sem=S.sent)
-
-    units = [(0, 0), (1, 0), (2, 0), (0, 1), (1, 1), (2, 1)] + [(j, h) for j in range(3, 8) for h in (1, 0)]
-    nu = len(units)
     sbank = [T.s0, T.s1, T.s2, T.s3]
-    oacc = [[T.o0, T.o1], [T.o2, T.o3]]
-    seen = set()
-    first = {0: min(u for u in range(nu) if units[u][1] == 0), 1: min(u for u in range(nu) if units[u][1] == 1)}
-    last = {0: max(u for u in range(nu) if units[u][1] == 0), 1: max(u for u in range(nu) if units[u][1] == 1)}
+    if is_rank:
+        runs = [(pos * P, pos * P + P, T.qin[:, hc:hc + P]), (pos * P + P, 512, T.qb[:, pos * P + P:512])]
+        if pos > 0:
+            runs.append((0, pos * P, T.qb[:, 0:pos * P]))
+    else:
+        runs = [(0, 512, T.qb[:, 0:512])]
 
-    def twait(name, val):
-        if name not in seen:
-            seen.add(name)
-            g.tensor.wait_ge(S[name], val)
-
-    def k_of(j, h):
+    def twaits(x, j):
         if j == 0:
-            return T.kin[:, mycol + P * h:mycol + P * h + P]
-        return T.kland[:, (j - 1) * W + P * h:(j - 1) * W + P * h + P]
+            if is_rank:
+                g.tensor.wait_ge(S["ld" + x], 32)
+            g.tensor.wait_ge(S["n" + x], n_near)
+        if j == 2:
+            g.tensor.wait_ge(S["f" + x], n_far[x])
 
-    def v_of(j, h):
-        if j == 0:
-            return T.vin[:, mycol + P * h:mycol + P * h + P]
-        return T.vland[:, (j - 1) * W + P * h:(j - 1) * W + P * h + P]
+    twaits("q", 0)
+    twaits("q", 2)
+    for j in range(4):
+        twaits("k", j)
+        k_ap = T.kin[:, hc:hc + P] if (is_rank and j == pos) else T.kb[:, j * P:j * P + P]
+        for c0, c1, q_ap in runs:
+            g.tensor.matmul(sbank[j][:, c0:c1], k_ap, q_ap, True, True).then_inc(S["sd%d" % j], 1)
+    for j in range(4):
+        twaits("v", j)
+        v_ap = T.vin[:, hc:hc + P] if (is_rank and j == pos) else T.vb[:, j * P:j * P + P]
+        g.tensor.wait_ge(S["rd%d" % j], 1)
+        g.tensor.matmul(T.o[:, 0:512], v_ap, T.ssb[:, 512 * j:512 * j + 512], j == 0, j == 3).then_inc(S.od, 1)
 
-    def q_of(slot, h):
-        if me["slots"][slot] == core:
-            return T.qin[:, mycol + P * h:mycol + P * h + P]
-        c0 = 0 if slot < 2 else (slot - 1) * W
-        return T.qland[:, c0 + P * h:c0 + P * h + P]
-
-    def emit_s(u):
-        j, half = units[u]
-        b = u % NB
-        if j == 0:
-            twait("ldB", 48)
-        else:
-            twait("akv%d" % j, 2 * KV_ENG[j])
-        if half == 0:
-            twait("ldB", 48)
-            twait("aqp", 2)
-        else:
-            twait("aqc", 4)
-        for h in (0, 1):
-            for s in (0, 1):
-                c0 = W * h + P * s
-                g.tensor.matmul(sbank[b][:, c0:c0 + P], k_of(j, h), q_of(2 * half + s, h), True, True).then_inc(S["sd%d" % b], 1)
-
-    def emit_o(u):
-        j, half = units[u]
-        b = u % NB
-        g.tensor.wait_ge(S["rd%d" % b], u // NB + 1)
-        for h in (0, 1):
-            g.tensor.matmul(oacc[half][h][:, 0:W], v_of(j, h), T.ssb[:, 512 * b + W * h:512 * b + W * h + W],
-                            u == first[half], u == last[half]).then_inc(S["od%d" % b], 1)
-
-    emit_s(0)
-    for u in range(nu):
-        if u + 1 < nu:
-            emit_s(u + 1)
-        emit_o(u)
-
+    g.vector.memset(T.zeros[:, :], 0.0).then_inc(S.zs, 1)
     g.vector.wait_ge(S.zs, 1)
-    for u in range(nu):
-        b = u % NB
-        g.vector.wait_ge(S["sd%d" % b], 4 * (u // NB + 1))
-        if u >= NB:
-            g.vector.wait_ge(S["od%d" % b], 2 * (u // NB))
-        g.vector.tensor_tensor(T.ssb[:, 512 * b:512 * b + 512], sbank[b][:, :], T.zeros[:, :], AluOpType.max).then_inc(S["rd%d" % b], 1)
-    for u in range(nu - NB, nu - 1):
-        g.vector.wait_ge(S["od%d" % (u % NB)], 2 * (u // NB + 1))
-    for s in (0, 1):
-        for h in (0, 1):
-            g.vector.tensor_copy(T.osb[:, W * (s + 1) + P * h:W * (s + 1) + P * h + P], oacc[1][h][:, P * s:P * s + P]).then_inc(S.ocf, 1)
-    g.vector.wait_ge(S["od%d" % ((nu - 1) % NB)], 2 * ((nu - 1) // NB + 1))
-    for h in (0, 1):
-        g.vector.tensor_copy(T.osb[:, P * h:P * h + P], oacc[0][h][:, P * (1 - pos):P * (1 - pos) + P]).then_inc(S.ocp, 1)
-    for h in (0, 1):
-        g.vector.tensor_copy(T.ybuf[:, mycol + P * h:mycol + P * h + P], oacc[0][h][:, P * pos:P * pos + P]).then_inc(S.oco, 1)
+    for j in range(4):
+        g.vector.wait_ge(S["sd%d" % j], len(runs))
+        g.vector.tensor_tensor(T.ssb[:, 512 * j:512 * j + 512], sbank[j][:, :], T.zeros[:, :], AluOpType.max).then_inc(S["rd%d" % j], 1)
+    g.vector.wait_ge(S.od, 4)
+    ncopy = 0
+    for c0, c1, _ in (runs[1:] if is_rank else runs):
+        g.vector.tensor_copy(T.osb[:, c0:c1], T.o[:, c0:c1]).then_inc(S.oc, 1)
+        ncopy += 1
+    if is_rank:
+        g.vector.tensor_copy(T.ya[:, hc:hc + P], T.o[:, pos * P:pos * P + P]).then_inc(S.own, 1)
 
-    g.wait_ge(S.ocf, 4)
-    g.remote_dma_fused([xfer(C[0], T.osb[:, W:2 * W], T.ybuf[:, mycol:mycol + W], off[0:4], S.ayc),
-                        xfer(C[1], T.osb[:, 2 * W:3 * W], T.ybuf[:, mycol:mycol + W], off[4:8], S.ayc)], local_sem=S.sent)
-    g.wait_ge(S.ocp, 2)
-    g.remote_dma_fused([xfer(partner, T.osb[:, 0:W], T.ybuf[:, mycol:mycol + W], on[0:4], S.ayp)], local_sem=S.sent)
+    back_eng = [[off[1], off[3]], [off[5], off[7]], [off[0], off[2]], [off[4], off[6]]]
+    ay = S["ay%d" % (head // 4)]
+    tr = []
+    for s in range(4):
+        if askers[s] != core:
+            dst = T.ya if s < 2 else T.yb
+            tr.append(xfer(askers[s], T.osb[:, s * P:s * P + P], dst[:, hc:hc + P], back_eng[s], ay))
+    g.wait_ge(S.oc, ncopy)
+    g.remote_dma_fused(tr, local_sem=S.sent)
 
-    g.sync.wait_ge(S.oco, 2)
-    g.sync.wait_ge(S.ayp, 4)
-    g.sync.dma_start(T.y[:, near:near + 512], T.ybuf[:, near:near + 512]).then_inc(S.st, 16)
-    g.scalar.wait_ge(S.ayc, 8)
-    g.scalar.dma_start(T.y[:, far:far + 512], T.ybuf[:, far:far + 512]).then_inc(S.st, 16)
-
+    if is_rank:
+        g.vector.wait_ge(S.own, 1)
+        for hf, queue in ((0, g.sync), (1, g.scalar)):
+            n = sum(2 for h in range(4 * hf, 4 * hf + 4) if me["work"][h] != core) + 2 * 4
+            c = slice(512 * hf, 512 * hf + 512)
+            g.vector.wait_ge(S["ay%d" % hf], n)
+            g.vector.tensor_tensor(T.ys[:, c], T.ya[:, c], T.yb[:, c], AluOpType.add).then_inc(S["yd%d" % hf], 1)
+            queue.wait_ge(S["yd%d" % hf], 1)
+            queue.dma_start(T.y[:, c], T.ys[:, c]).then_inc(S.st, 16)
+        g.wait_ge(S.st, 32)
     g.wait_ge(S.sent, sent[0])
-    g.wait_ge(S.st, 32)

@@ -27,6 +27,7 @@ SEMAPHORES = (["ldq", "ldk", "ldv", "sent", "zs", "od", "oc", "own", "ay0", "ay1
               + ["sd%d" % j for j in range(4)] + ["rd%d" % j for j in range(4)])
 
 E_DEAL, E_OWN = 2, 1
+LOAD_PARTS = 2
 
 
 def _bits(m):
@@ -70,9 +71,14 @@ def rank_program(g, core, T, topo):
     is_rank = T.rank_of(core) is not None
     pos = me["ranks"].index(core) if is_rank else None
     S = T.sem
-    askers = me["ranks"] + mate["ranks"]
-    other = {"q": mate, "k": cable, "v": cable}
+
+    def other(x, h):
+        q_by_switch = (h // 2) % 2 == 0
+        return mate if (x == "q") == q_by_switch else cable
+
+    askers = me["ranks"] + other("q", head)["ranks"]
     land = {"q": T.qb, "k": T.kb, "v": T.vb}
+    n_ld = 16 * LOAD_PARTS
 
     off = _bits(topo.mask(core, mate["ranks"][0]) & topo.mask(core, cable["ranks"][0]))
     on = [e for e in _bits(topo.mask(core, [c for c in me["work"] if c != core][0])) if e not in off]
@@ -87,9 +93,11 @@ def rank_program(g, core, T, topo):
     if is_rank:
         src = {"q": T.qin, "k": T.kin, "v": T.vin}
         inp = {"q": T.q, "k": T.k, "v": T.v}
+        w = 1024 // LOAD_PARTS
         for x in "qkv":
-            g.sync.dma_start(src[x][:, 0:512], inp[x][:, 0:512]).then_inc(S["ld" + x], 16)
-            g.scalar.dma_start(src[x][:, 512:1024], inp[x][:, 512:1024]).then_inc(S["ld" + x], 16)
+            for i in range(LOAD_PARTS):
+                queue = g.sync if i < LOAD_PARTS // 2 else g.scalar
+                queue.dma_start(src[x][:, w * i:w * i + w], inp[x][:, w * i:w * i + w]).then_inc(S["ld" + x], 16)
         near, far = slice(pos * P, pos * P + P), slice((2 + pos) * P, (2 + pos) * P + P)
         duo = [(off + on)[2 * i:2 * i + 2] for i in range(8)]
         same = [c for c in me["work"] if c != core and topo.die(c) == topo.die(core)]
@@ -100,7 +108,7 @@ def rank_program(g, core, T, topo):
             rest = [duo[i] for i in range(8) if i not in (a, b)]
             tr = []
             for i, h in enumerate(lone):
-                tr.append(xfer(other[x]["work"][h], src[x][:, P * h:P * h + P], land[x][:, far], [duo[(a, b)[i]][side]], S["f" + x]))
+                tr.append(xfer(other(x, h)["work"][h], src[x][:, P * h:P * h + P], land[x][:, far], [duo[(a, b)[i]][side]], S["f" + x]))
             plan = [(cross[3], [duo[a][1 - side], duo[b][1 - side]])]
             for i in range(3):
                 plan.append((same[i], [rest[2 * i][0], rest[2 * i + 1][0]]))
@@ -108,16 +116,16 @@ def rank_program(g, core, T, topo):
             for dst, eng in plan:
                 h = me["work"].index(dst)
                 tr.append(xfer(dst, src[x][:, P * h:P * h + P], land[x][:, near], eng, S["n" + x]))
-            g.wait_ge(S["ld" + x], 32)
+            g.wait_ge(S["ld" + x], n_ld)
             g.remote_dma_fused(tr, local_sem=S.sent)
     else:
         for x in "qkv":
             g.wait_ge(S["n" + x], 2 * E_DEAL)
-            g.remote_dma_fused([xfer(other[x]["work"][head], land[x][:, 0:2 * P], land[x][:, 2 * P:4 * P], off, S["f" + x])],
+            g.remote_dma_fused([xfer(other(x, head)["work"][head], land[x][:, 0:2 * P], land[x][:, 2 * P:4 * P], off, S["f" + x])],
                                local_sem=S.sent)
 
     n_near = E_DEAL * len([r for r in me["ranks"] if r != core])
-    n_far = {x: (2 * E_OWN if other[x]["work"][head] in cores else len(off)) for x in "qkv"}
+    n_far = {x: (2 * E_OWN if other(x, head)["work"][head] in cores else len(off)) for x in "qkv"}
 
     sbank = [T.s0, T.s1, T.s2, T.s3]
     if is_rank:
@@ -130,7 +138,7 @@ def rank_program(g, core, T, topo):
     def twaits(x, j):
         if j == 0:
             if is_rank:
-                g.tensor.wait_ge(S["ld" + x], 32)
+                g.tensor.wait_ge(S["ld" + x], n_ld)
             g.tensor.wait_ge(S["n" + x], n_near)
         if j == 2:
             g.tensor.wait_ge(S["f" + x], n_far[x])

from concourse.bass import DstId, RemoteDMATransfer
from concourse.mybir import AluOpType

WORLD = 512
P = 128
NH = 8

SCRATCH = {
    "qin": ("sbuf", [128, 1024], "bfloat16"),
    "kin": ("sbuf", [128, 1024], "bfloat16"),
    "vin": ("sbuf", [128, 1024], "bfloat16"),
    "qb": ("sbuf", [128, 4 * P], "bfloat16"),
    "kb": ("sbuf", [128, 4 * P], "bfloat16"),
    "vb": ("sbuf", [128, 4 * P], "bfloat16"),
    "ssb": ("sbuf", [128, 4 * 512], "bfloat16"),
    "zeros": ("sbuf", [128, 512], "float32"),
    "osb": ("sbuf", [128, 4 * P], "bfloat16"),
    "ya": ("sbuf", [128, 1024], "bfloat16"),
    "yb": ("sbuf", [128, 1024], "bfloat16"),
    "ys": ("sbuf", [128, 1024], "bfloat16"),
    "s0": ("psum", [128, 512], "float32"), "s1": ("psum", [128, 512], "float32"),
    "s2": ("psum", [128, 512], "float32"), "s3": ("psum", [128, 512], "float32"),
    "o": ("psum", [128, 512], "float32"),
}
SEMAPHORES = (["ldq", "ldk", "ldv", "sent", "zs", "od", "oc", "own", "ay0", "ay1", "yd0", "yd1", "st"]
              + ["n" + x for x in "qkv"] + ["f" + x for x in "qkv"]
              + ["sd%d" % j for j in range(4)] + ["rd%d" % j for j in range(4)])

E_DEAL, E_OWN = 2, 1
LOAD_PARTS = 2


def _bits(m):
    return [e for e in range(m.bit_length()) if (m >> e) & 1]


def _mask(es):
    m = 0
    for e in es:
        m |= 1 << e
    return m


def _layout(cores, topo):
    L = {}
    for H in sorted({topo.host(c) for c in cores}):
        ranks = [c for c in cores if topo.host(c) == H]
        r0 = ranks[0]
        chip = [c for c in range(WORLD) if topo.host(c) == H and topo.chip(c) == topo.chip(r0)]
        a = [c for c in chip if topo.die(c) == topo.die(r0)]
        b = [c for c in chip if topo.die(c) != topo.die(r0)]
        work = []
        for x, y in zip(a, b):
            work += [x, y]
        mate = [topo.host(d) for d in cores if topo.same_plane(r0, d)][0]
        cable = [topo.host(d) for d in cores if topo.rack(topo.host(d)) != topo.rack(H) and topo.may_write(r0, d)][0]
        L[H] = {"ranks": ranks, "work": work, "mate": mate, "cable": cable}
    return L


def rank_program(g, core, T, topo):
    cores = list(T.cores)
    L = _layout(cores, topo)
    H = topo.host(core)
    if H not in L or core not in L[H]["work"]:
        return
    me = L[H]
    mate, cable = L[me["mate"]], L[me["cable"]]
    head = me["work"].index(core)
    hc = P * head
    is_rank = T.rank_of(core) is not None
    pos = me["ranks"].index(core) if is_rank else None
    S = T.sem

    def other(x, h):
        q_by_switch = (h // 2) % 2 == 0
        return mate if (x == "q") == q_by_switch else cable

    askers = me["ranks"] + other("q", head)["ranks"]
    land = {"q": T.qb, "k": T.kb, "v": T.vb}
    n_ld = 16 * LOAD_PARTS

    off = _bits(topo.mask(core, mate["ranks"][0]) & topo.mask(core, cable["ranks"][0]))
    on = [e for e in _bits(topo.mask(core, [c for c in me["work"] if c != core][0])) if e not in off]
    sent = [0]

    def xfer(dst, src_ap, dst_ap, engines, sem):
        rid, pid = topo.addr(dst, core)
        sent[0] += len(engines)
        return RemoteDMATransfer(dst_ids=[DstId(rid=rid, pnc=pid)], dma_engine_mask=_mask(engines), remote_sem=sem,
                                 src=src_ap, dst=dst_ap)

    if is_rank:
        src = {"q": T.qin, "k": T.kin, "v": T.vin}
        inp = {"q": T.q, "k": T.k, "v": T.v}
        w = 1024 // LOAD_PARTS
        for x in "qkv":
            for i in range(LOAD_PARTS):
                queue = g.sync if i < LOAD_PARTS // 2 else g.scalar
                queue.dma_start(src[x][:, w * i:w * i + w], inp[x][:, w * i:w * i + w]).then_inc(S["ld" + x], 16)
        near, far = slice(pos * P, pos * P + P), slice((2 + pos) * P, (2 + pos) * P + P)
        duo = [(off + on)[2 * i:2 * i + 2] for i in range(8)]
        same = [c for c in me["work"] if c != core and topo.die(c) == topo.die(core)]
        cross = [c for c in me["work"] if topo.die(c) != topo.die(core)]
        lone = [h for h in range(NH) if me["work"][h] in cores]
        for ci, x in enumerate("qkv"):
            a, b, side = [(0, 1, 0), (2, 3, 0), (0, 1, 1)][ci]
            rest = [duo[i] for i in range(8) if i not in (a, b)]
            tr = []
            for i, h in enumerate(lone):
                tr.append(xfer(other(x, h)["work"][h], src[x][:, P * h:P * h + P], land[x][:, far], [duo[(a, b)[i]][side]], S["f" + x]))
            plan = [(cross[3], [duo[a][1 - side], duo[b][1 - side]])]
            for i in range(3):
                plan.append((same[i], [rest[2 * i][0], rest[2 * i + 1][0]]))
                plan.append((cross[i], [rest[2 * i][1], rest[2 * i + 1][1]]))
            for dst, eng in plan:
                h = me["work"].index(dst)
                tr.append(xfer(dst, src[x][:, P * h:P * h + P], land[x][:, near], eng, S["n" + x]))
            g.wait_ge(S["ld" + x], n_ld)
            g.remote_dma_fused(tr, local_sem=S.sent)
    else:
        for x in "qkv":
            g.wait_ge(S["n" + x], 2 * E_DEAL)
            g.remote_dma_fused([xfer(other(x, head)["work"][head], land[x][:, 0:2 * P], land[x][:, 2 * P:4 * P], off, S["f" + x])],
                               local_sem=S.sent)

    n_near = E_DEAL * len([r for r in me["ranks"] if r != core])
    n_far = {x: (2 * E_OWN if other(x, head)["work"][head] in cores else len(off)) for x in "qkv"}

    sbank = [T.s0, T.s1, T.s2, T.s3]
    if is_rank:
        runs = [(pos * P, pos * P + P, T.qin[:, hc:hc + P]), (pos * P + P, 512, T.qb[:, pos * P + P:512])]
        if pos > 0:
            runs.append((0, pos * P, T.qb[:, 0:pos * P]))
    else:
        runs = [(0, 512, T.qb[:, 0:512])]

    def twaits(x, j):
        if j == 0:
            if is_rank:
                g.tensor.wait_ge(S["ld" + x], n_ld)
            g.tensor.wait_ge(S["n" + x], n_near)
        if j == 2:
            g.tensor.wait_ge(S["f" + x], n_far[x])

    twaits("q", 0)
    twaits("q", 2)
    for j in range(4):
        twaits("k", j)
        k_ap = T.kin[:, hc:hc + P] if (is_rank and j == pos) else T.kb[:, j * P:j * P + P]
        for c0, c1, q_ap in runs:
            g.tensor.matmul(sbank[j][:, c0:c1], k_ap, q_ap, True, True).then_inc(S["sd%d" % j], 1)
    for j in range(4):
        twaits("v", j)
        v_ap = T.vin[:, hc:hc + P] if (is_rank and j == pos) else T.vb[:, j * P:j * P + P]
        g.tensor.wait_ge(S["rd%d" % j], 1)
        g.tensor.matmul(T.o[:, 0:512], v_ap, T.ssb[:, 512 * j:512 * j + 512], j == 0, j == 3).then_inc(S.od, 1)

    g.vector.memset(T.zeros[:, :], 0.0).then_inc(S.zs, 1)
    g.vector.wait_ge(S.zs, 1)
    for j in range(4):
        g.vector.wait_ge(S["sd%d" % j], len(runs))
        g.vector.tensor_tensor(T.ssb[:, 512 * j:512 * j + 512], sbank[j][:, :], T.zeros[:, :], AluOpType.max).then_inc(S["rd%d" % j], 1)
    g.vector.wait_ge(S.od, 4)
    ncopy = 0
    for c0, c1, _ in (runs[1:] if is_rank else runs):
        g.vector.tensor_copy(T.osb[:, c0:c1], T.o[:, c0:c1]).then_inc(S.oc, 1)
        ncopy += 1
    if is_rank:
        g.vector.tensor_copy(T.ya[:, hc:hc + P], T.o[:, pos * P:pos * P + P]).then_inc(S.own, 1)

    back_eng = [[off[1], off[3]], [off[5], off[7]], [off[0], off[2]], [off[4], off[6]]]
    ay = S["ay%d" % (head // 4)]
    tr = []
    for s in range(4):
        if askers[s] != core:
            dst = T.ya if s < 2 else T.yb
            tr.append(xfer(askers[s], T.osb[:, s * P:s * P + P], dst[:, hc:hc + P], back_eng[s], ay))
    g.wait_ge(S.oc, ncopy)
    g.remote_dma_fused(tr, local_sem=S.sent)

    if is_rank:
        g.vector.wait_ge(S.own, 1)
        for hf, queue in ((0, g.sync), (1, g.scalar)):
            n = sum(2 for h in range(4 * hf, 4 * hf + 4) if me["work"][h] != core) + 2 * 4
            c = slice(512 * hf, 512 * hf + 512)
            g.vector.wait_ge(S["ay%d" % hf], n)
            g.vector.tensor_tensor(T.ys[:, c], T.ya[:, c], T.yb[:, c], AluOpType.add).then_inc(S["yd%d" % hf], 1)
            queue.wait_ge(S["yd%d" % hf], 1)
            queue.dma_start(T.y[:, c], T.ys[:, c]).then_inc(S.st, 16)
        g.wait_ge(S.st, 32)
    g.wait_ge(S.sent, sent[0])
